import numpy as np
import ml_dtypes


def mxq(x, axis, fmt="e4m3"):
    dtype, down = {"e4m3": (ml_dtypes.float8_e4m3fn, 7), "e5m2": (ml_dtypes.float8_e5m2, 14)}[fmt]
    v = np.moveaxis(np.asarray(x, np.float32).astype(ml_dtypes.bfloat16).astype(np.float64), axis, -1)
    blocks = v.reshape(v.shape[:-1] + (-1, 32))
    amax = np.abs(blocks).max(-1, keepdims=True)
    byte = np.maximum(np.where(amax > 0, np.frexp(amax)[1] - 1 + 127, 0) - down, 1)
    scale = np.exp2(byte - 127.0)
    codes = (blocks / scale).astype(np.float32).astype(dtype).astype(np.float64)
    return np.moveaxis((codes * scale).reshape(v.shape), -1, axis)


WIDE = False


def mx_kscale(k):
    if not WIDE:
        return np.ones(k)
    levels = np.array([10, -10, 5, -5, 0])
    if k % 512:
        return np.exp2(np.random.permutation(np.resize(levels, k // 32))).repeat(32)
    a = np.empty((k // 512, 16))
    for p in range(k // 512):
        a[p, :8] = np.random.permutation(np.resize(levels, 8))
        for g in range(8):
            far = levels[np.abs(levels - a[p, g]) >= 10]
            a[p, g + 8] = far[np.random.randint(len(far))]
    return np.exp2(a.ravel()).repeat(32)


def f64(x):
    return np.asarray(x).astype(np.float64)


def striped(idx):
    return np.tile(idx.reshape(-1, 16).T, (8, 1)).astype(np.uint16)


def unstriped(offs):
    return offs[:16].T.reshape(-1).astype(np.int64)


def striped8(idx):
    return np.concatenate([x.reshape(-1, 16).T for x in idx]).astype(np.uint16)


def runs(offs, k):
    lists = np.stack([offs[16 * r : 16 * r + 16].T.reshape(-1) for r in range(8)]).astype(np.int64)
    return lists[np.arange(k) % 512 // 64]


def pack_weight(w):
    k, n = w.shape
    w = f64(np.asarray(w, np.float32).astype(ml_dtypes.bfloat16)).reshape(k // 32, 32, n)
    amax = np.abs(w).max(1)
    byte = np.clip(np.where(amax > 0, np.frexp(amax)[1] - 1 + 127 - 7, 1), 1, 254)
    scaled = (w * np.exp2(127.0 - byte)[:, None, :]).reshape(k, n).astype(np.float32)
    words = np.ascontiguousarray(scaled.reshape(k // 512, 128, 4, n).transpose(0, 1, 3, 2)).astype(ml_dtypes.float8_e4m3fn).view(np.uint8)
    return words, np.ascontiguousarray(byte.astype(np.uint8).reshape(k // 512, 16, n))


def unpack_weight(words, scales):
    g, p, n, _ = words.shape
    vals = np.ascontiguousarray(words).view(ml_dtypes.float8_e4m3fn).astype(np.float64) * np.repeat(np.exp2(scales.astype(np.float64) - 127.0), 8, axis=1)[..., None]
    return vals.transpose(0, 1, 3, 2).reshape(g * 512, n)


K, T, S, N, H, W = 512, 2048, 512, 512, 512, 256


def setup_inputs():
    n = np.random.standard_normal
    s = mx_kscale(K)[:, None]
    u = mx_kscale(S)
    packed_xT = pack_weight(n((K, T)) * s)
    perm = np.stack([np.random.permutation(H) for _ in range(8)])
    return {
        "x_words": packed_xT[0],
        "x_scales": packed_xT[1],
        "wa": (n((K, H)) / np.sqrt(K) / s).astype(np.float32),
        "wb": (n((K, N)) / np.sqrt(K) / s).astype(np.float32),
        "gt": (np.random.uniform(0.5, 1.5, (S, 1)) * u[:, None]).astype(np.float32),
        "gi": (np.random.uniform(0.5, 1.5, (S, 1)) / u[:, None]).astype(np.float32),
        "offs": striped(np.random.permutation(T)[:S]),
        "two": striped(np.random.permutation(T)[:S]),
        "n1": striped8(perm[:, :W]),
        "n2": striped8(perm[:, W:]),
        "n3": striped8(np.stack([np.random.permutation(N) for _ in range(8)])),
        "n4": striped8(np.stack([np.random.permutation(N) for _ in range(8)])),
        "n5": striped8(np.stack([np.random.permutation(N) for _ in range(8)])),
        "n6": striped8(np.stack([np.random.permutation(N) for _ in range(8)])),
        "n7": striped8(np.stack([np.random.permutation(N) for _ in range(8)])),
    }


def reference(x_words, x_scales, wa, wb, gt, gi, offs, two, n1, n2, n3, n4, n5, n6, n7):
    xq = unpack_weight(x_words, x_scales)[:, unstriped(offs)]
    a = xq.T @ mxq(f64(wa), 0, "e4m3")
    pa = a[np.arange(S)[:, None], runs(n1, S)]
    pb = a[np.arange(S)[:, None], runs(n2, S)]
    rb = pa * pb
    ra = pa + pb
    ds = np.zeros((S, H))
    ds[np.arange(S)[:, None], runs(n1, S)] = ra
    dt = ds.copy()
    dt[np.arange(S)[:, None], runs(n2, S)] = rb
    z = f64(gt) * dt
    x_two = unpack_weight(x_words, x_scales)[:, unstriped(two)]
    b = x_two.T @ mxq(f64(wb), 0, "e4m3")
    z2 = f64(gi) * (b + b[np.arange(S)[:, None], runs(n3, S)] - (np.maximum(b[np.arange(S)[:, None], runs(n4, S)], b[np.arange(S)[:, None], runs(n5, S)])))
    cv = 0.0625 * ((mxq(z, 0, "e4m3").T @ mxq(z2, 0, "e4m3")))
    return 0.75 * (cv[np.arange(H)[:, None], runs(n6, H)] + cv[np.arange(H)[:, None], runs(n7, H)]) - cv

@@ -1,0 +1,239 @@
+from contextlib import ExitStack
+
+import concourse.mybir as mybir
+from concourse.masks import make_identity
+
+K, T, S, N, H = 512, 2048, 512, 512, 512
+FLOPS = 2 * K * S * H + 2 * K * S * N + 2 * S * H * N
+
+F32 = mybir.dt.float32
+BF16 = mybir.dt.bfloat16
+I32 = mybir.dt.int32
+U32 = mybir.dt.uint32
+U16 = mybir.dt.uint16
+U8 = mybir.dt.uint8
+FP8X4 = mybir.dt.float8_e4m3fn_x4
+ADD = mybir.AluOpType.add
+SUB = mybir.AluOpType.subtract
+MULT = mybir.AluOpType.mult
+MAX = mybir.AluOpType.max
+COPY = mybir.ActivationFunctionType.Copy
+
+P = 128
+PACK = 4
+WIDE = 1024
+HALF = 256
+
+
+def tile_picked_mombbondtrimlap_none_p_kernel(
+    tc, x_words, x_scales, wa, wb, gt, gi, offs, two, n1, n2, n3, n4, n5, n6, n7, out
+):
+    nc = tc.nc
+    with ExitStack() as ctx:
+        keep = ctx.enter_context(tc.tile_pool(name="keep", bufs=1))
+        ring = ctx.enter_context(tc.tile_pool(name="ring", bufs=2))
+        psum = ctx.enter_context(tc.psum_pool(name="psum", bufs=8))
+
+        def load_list(src, name):
+            tile = keep.tile(list(src.shape), U16, name=name)
+            nc.sync.dma_start(tile[:], src)
+            return tile
+
+        def load_weight_half(w, half, name):
+            raw = keep.tile([P, PACK, HALF], F32, name=name)
+            nc.sync.dma_start(raw[:], w.rearrange("(p j) n -> p j n", j=PACK)[:, :, half * HALF : (half + 1) * HALF])
+            return raw
+
+        def round_weight_half(raw, name):
+            grouped = keep.tile([P, HALF, PACK], BF16, name=name, tag=name, align_bytes=64)
+            nc.scalar.copy(
+                grouped[:].rearrange("p (c i) j -> p c j i", i=4),
+                raw[:].rearrange("p j (c i) -> p c j i", i=4),
+            )
+            return grouped
+
+        def quantise(codes, scales, grouped):
+            nc.vector.quantize_mx(out=codes.bitcast(FP8X4), scales=scales, in_=grouped)
+
+        def pick_scales(lst, name, tag):
+            picked = keep.tile([P, S], U8, name=name + "_picked", tag=tag, align_bytes=64)
+            nc.vector.tensor_copy(picked[:], scale_table[:].indirect(lst[:]))
+            return picked
+
+        def deal_scales(picked, name):
+            dealt = keep.tile([P, S], U8, name=name + "_dealt", align_bytes=64)
+            nc.vector.tensor_copy(
+                dealt[:].bitcast(I32).rearrange("p (t q w) -> p t q w", t=PACK, w=2),
+                picked[:].bitcast(I32).rearrange("p (q t w) -> p t q w", t=PACK, w=2),
+            )
+            return dealt
+
+        def pick_words(lst, name):
+            picked = keep.tile([P, S], U32, name=name, align_bytes=64)
+            nc.vector.tensor_copy(
+                picked[:].rearrange("p (t q r) -> p q t r", t=PACK, r=8),
+                word_table[:].bitcast(U32).indirect(lst[:]),
+            )
+            return picked
+
+        def product(lhs_codes, lhs_scales, rhs_codes, rhs_scales, t, rhs_cols=slice(0, N)):
+            bank = psum.tile([P, N], F32, name="bank")
+            cols = slice(t * P, (t + 1) * P)
+            acc = bank[:, : rhs_cols.stop - rhs_cols.start]
+            nc.tensor.matmul_mx(
+                out=acc,
+                lhsT=lhs_codes[:, cols].bitcast(FP8X4),
+                lhsT_scale=lhs_scales[:, cols],
+                rhs=rhs_codes[:, rhs_cols].bitcast(FP8X4),
+                rhs_scale=rhs_scales[:, rhs_cols],
+                start=True,
+                stop=True,
+            )
+            return acc
+
+        scale_table = keep.tile([P, T], U8, name="scale_table")
+        nc.gpsimd.memset(scale_table[:].bitcast(I32), 0)
+        two_l = load_list(two, "two_l")
+        word_table = keep.tile([P, T], I32, name="word_table")
+        nc.sync.dma_start(word_table[:], x_words[0].rearrange("p n j -> p (n j)").bitcast(I32))
+        offs_l = load_list(offs, "offs_l")
+        for q in range(4):
+            nc.sync.dma_start(
+                scale_table[32 * q : 32 * q + 4, :].bitcast(I32), x_scales[0][4 * q : 4 * q + 4, :].bitcast(I32)
+            )
+        wb_raw = [load_weight_half(wb, h, "wb_raw%d" % h) for h in range(2)]
+        n3_l = load_list(n3, "n3_l")
+        n4_l = load_list(n4, "n4_l")
+        n5_l = load_list(n5, "n5_l")
+        wa_raw = [load_weight_half(wa, h, "wa_raw%d" % h) for h in range(2)]
+        gate_rows = keep.tile([P, P], F32, name="gate_rows")
+        nc.gpsimd.memset(gate_rows[:], 0.0)
+        for first, g in ((0, gt), (PACK, gi)):
+            nc.sync.dma_start(
+                gate_rows[first : first + PACK, :].rearrange("t (q r) -> t q r", r=8),
+                g.rearrange("(q t r) o -> t q (r o)", t=PACK, r=8),
+            )
+        n1_l = load_list(n1, "n1_l")
+        n2_l = load_list(n2, "n2_l")
+        n6_l = load_list(n6, "n6_l")
+        n7_l = load_list(n7, "n7_l")
+        ident = keep.tile([P, P], F32, name="ident")
+        make_identity(nc, ident[:])
+
+        windows = [keep.tile([P, WIDE], F32, name="window%d" % t) for t in range(PACK)]
+        for t in range(PACK):
+            nc.vector.memset(windows[t][:, N:], 0.0)
+
+        halves = [slice(h * HALF, (h + 1) * HALF) for h in range(2)]
+        two_words = pick_words(two_l, "two_w")
+        offs_words = pick_words(offs_l, "offs_w")
+        two_sp = pick_scales(two_l, "two_s", "two_s_picked")
+        two_scales = deal_scales(two_sp, "two_s")
+        wb_codes = keep.tile([P, N], U32, name="wb_codes", align_bytes=64)
+        wb_scales = keep.tile([P, N], U8, name="wb_scales", align_bytes=64)
+        b_plain = [keep.tile([P, N], F32, name="b_plain%d" % t) for t in range(PACK)]
+        wb_bf = [round_weight_half(wb_raw[h], "wb_bf%d" % h) for h in range(2)]
+        for h in range(2):
+            quantise(wb_codes[:, halves[h]], wb_scales[:, halves[h]], wb_bf[h][:].rearrange("p c j -> p (c j)"))
+            acc = product(two_words, two_scales, wb_codes, wb_scales, 0, halves[h])
+            nc.scalar.copy(windows[0][:, halves[h]], acc)
+            nc.scalar.copy(b_plain[0][:, halves[h]], acc)
+        offs_sp = pick_scales(offs_l, "offs_s", "wb_bf1")
+        offs_scales = deal_scales(offs_sp, "offs_s")
+        for t in range(1, PACK):
+            acc = product(two_words, two_scales, wb_codes, wb_scales, t)
+            nc.scalar.copy(windows[t][:, :N], acc)
+            nc.scalar.copy(b_plain[t][:], acc)
+
+        gate_bank = psum.tile([P, N], F32, name="bank")
+        nc.tensor.transpose(gate_bank[:, :P], gate_rows[:], ident[:])
+        gt_col = keep.tile([P, PACK], F32, name="gt_col")
+        neg_gi_col = keep.tile([P, PACK], F32, name="neg_gi_col")
+        nc.scalar.copy(gt_col[:], gate_bank[:, :PACK])
+        nc.scalar.activation(neg_gi_col[:], gate_bank[:, PACK : 2 * PACK], COPY, scale=-1.0)
+
+        wa_bf = [round_weight_half(wa_raw[h], "wa_bf%d" % h) for h in range(2)]
+
+        z2_bf = keep.tile([P, N, PACK], BF16, name="z2_bf", align_bytes=64)
+        for pair in ((0, 1), (2, 3)):
+            u, v, w, m = {}, {}, {}, {}
+            for t in pair:
+                u[t] = ring.tile([P, N], F32, name="u")
+                nc.vector.tensor_tensor(u[t][:], windows[t][:].indirect(n3_l[:]), b_plain[t][:], ADD)
+            for t in pair:
+                v[t] = ring.tile([P, N], F32, name="v")
+                nc.vector.tensor_tensor(v[t][:], windows[t][:].indirect(n4_l[:]), u[t][:], SUB)
+            for t in pair:
+                w[t] = ring.tile([P, N], F32, name="w")
+                nc.vector.tensor_tensor(w[t][:], windows[t][:].indirect(n5_l[:]), u[t][:], SUB)
+            for t in pair:
+                m[t] = ring.tile([P, N], F32, name="m")
+                nc.vector.tensor_tensor(m[t][:], v[t][:], w[t][:], MAX)
+                nc.scalar.activation(z2_bf[:, :, t], m[t][:], COPY, scale=neg_gi_col[:, t : t + 1])
+            if pair[0] == 0:
+                wa_codes = keep.tile([P, H], U32, name="wa_codes", align_bytes=64)
+                wa_scales = keep.tile([P, H], U8, name="wa_scales", align_bytes=64)
+                for h in range(2):
+                    cols = slice(h * HALF, (h + 1) * HALF)
+                    quantise(wa_codes[:, cols], wa_scales[:, cols], wa_bf[h][:].rearrange("p c j -> p (c j)"))
+                a_rows = []
+                for t in range(PACK):
+                    bank = product(offs_words, offs_scales, wa_codes, wa_scales, t)
+                    rows = keep.tile([P, H], F32, name="a_rows%d" % t)
+                    nc.scalar.copy(rows[:], bank)
+                    a_rows.append(rows)
+
+        z_bf = [keep.tile([P, P, PACK], BF16, name="z_bf%d" % e, align_bytes=64) for e in range(PACK)]
+        for pair in ((0, 1), (2, 3)):
+            pa, pb, dt = {}, {}, {}
+            for t in pair:
+                pa[t] = ring.tile([P, HALF], F32, name="pa")
+                nc.vector.tensor_copy(pa[t][:], a_rows[t][:].indirect(n1_l[:]))
+                if t == PACK - 1:
+                    pb[t] = keep.tile([P, HALF], F32, name="pb_last", tag="late", align_bytes=64)
+                else:
+                    pb[t] = ring.tile([P, HALF], F32, name="pb")
+                nc.vector.tensor_copy(pb[t][:], a_rows[t][:].indirect(n2_l[:]))
+            for t in pair:
+                dt[t] = ring.tile([P, H], F32, name="dt")
+                nc.vector.tensor_tensor(dt[t][:].indirect(n1_l[:]), pa[t][:], pb[t][:], ADD)
+            for t in pair:
+                nc.vector.tensor_tensor(dt[t][:].indirect(n2_l[:]), pa[t][:], pb[t][:], MULT)
+                by_residue = dt[t][:].rearrange("p (m e) -> p e m", e=PACK)
+                for e in range(PACK):
+                    nc.scalar.activation(z_bf[e][:, :, t], by_residue[:, e, :], COPY, scale=gt_col[:, t : t + 1])
+
+        z2_codes = keep.tile([P, N], U32, name="z2_codes", tag="late", align_bytes=64)
+        z2_scales = keep.tile([P, N], U8, name="z2_scales", align_bytes=64)
+        quantise(z2_codes[:], z2_scales[:], z2_bf[:].rearrange("p c j -> p (c j)"))
+        z_codes = keep.tile([P, H], U32, name="z_codes", align_bytes=64)
+        z_scales = keep.tile([P, H], U8, name="z_scales", align_bytes=64)
+        neg_cv = [keep.tile([P, N], F32, name="neg_cv%d" % e) for e in range(PACK)]
+        for e in range(PACK):
+            cols = slice(e * P, (e + 1) * P)
+            quantise(z_codes[:, cols], z_scales[:, cols], z_bf[e][:].rearrange("p c j -> p (c j)"))
+            if e == 0:
+                left = product(z_codes, z_scales, z2_codes, z2_scales, e, halves[0])
+                right = product(z_codes, z_scales, z2_codes, z2_scales, e, halves[1])
+                nc.scalar.activation(windows[e][:, halves[0]], left, COPY, scale=0.75 * 0.0625)
+                nc.scalar.activation(neg_cv[e][:, halves[0]], left, COPY, scale=-0.0625)
+                nc.vector.tensor_scalar_mul(windows[e][:, halves[1]], right, 0.75 * 0.0625)
+                nc.vector.tensor_scalar_mul(neg_cv[e][:, halves[1]], right, -0.0625)
+            else:
+                acc = product(z_codes, z_scales, z2_codes, z2_scales, e)
+                nc.scalar.activation(windows[e][:, :N], acc, COPY, scale=0.75 * 0.0625)
+                nc.scalar.activation(neg_cv[e][:], acc, COPY, scale=-0.0625)
+
+        out_rows = out.rearrange("(m e) n -> e m n", e=PACK)
+        for pair in ((0, 1), (2, 3)):
+            part = {}
+            for e in pair:
+                part[e] = ring.tile([P, N], F32, name="part")
+                nc.vector.tensor_tensor(part[e][:], windows[e][:].indirect(n6_l[:]), neg_cv[e][:], ADD)
+            for e in pair:
+                pieces = halves if e == PACK - 1 else [slice(0, N)]
+                for cols in pieces:
+                    res = ring.tile([P, cols.stop - cols.start], F32, name="res", bufs=3)
+                    entries = n7_l[:, cols.start // 16 : cols.stop // 16]
+                    nc.vector.tensor_tensor(res[:], windows[e][:].indirect(entries), part[e][:, cols], ADD)
+                    nc.sync.dma_start(out_rows[e][:, cols], res[:])

@@ -16,8 +16,10 @@ FP8X4 = mybir.dt.float8_e4m3fn_x4
 ADD = mybir.AluOpType.add
 SUB = mybir.AluOpType.subtract
 MULT = mybir.AluOpType.mult
-MAX = mybir.AluOpType.max
+IS_GE = mybir.AluOpType.is_ge
 COPY = mybir.ActivationFunctionType.Copy
+ABS = mybir.ActivationFunctionType.Abs
+RELU = mybir.ActivationFunctionType.Relu
 
 P = 128
 PACK = 4
@@ -32,7 +34,7 @@ def tile_picked_mombbondtrimlap_none_p_kernel(
     with ExitStack() as ctx:
         keep = ctx.enter_context(tc.tile_pool(name="keep", bufs=1))
         ring = ctx.enter_context(tc.tile_pool(name="ring", bufs=2))
-        psum = ctx.enter_context(tc.psum_pool(name="psum", bufs=8))
+        psum = ctx.enter_context(tc.psum_pool(name="psum", bufs=4))
 
         def load_list(src, name):
             tile = keep.tile(list(src.shape), U16, name=name)
@@ -44,13 +46,11 @@ def tile_picked_mombbondtrimlap_none_p_kernel(
             nc.sync.dma_start(raw[:], w.rearrange("(p j) n -> p j n", j=PACK)[:, :, half * HALF : (half + 1) * HALF])
             return raw
 
-        def round_weight_half(raw, name):
-            grouped = keep.tile([P, HALF, PACK], BF16, name=name, tag=name, align_bytes=64)
+        def round_weight_half(raw, grouped):
             nc.scalar.copy(
-                grouped[:].rearrange("p (c i) j -> p c j i", i=4),
+                grouped.rearrange("p (c i) j -> p c j i", i=4),
                 raw[:].rearrange("p j (c i) -> p c j i", i=4),
             )
-            return grouped
 
         def quantise(codes, scales, grouped):
             nc.vector.quantize_mx(out=codes.bitcast(FP8X4), scales=scales, in_=grouped)
@@ -76,8 +76,8 @@ def tile_picked_mombbondtrimlap_none_p_kernel(
             )
             return picked
 
-        def product(lhs_codes, lhs_scales, rhs_codes, rhs_scales, t, rhs_cols=slice(0, N)):
-            bank = psum.tile([P, N], F32, name="bank")
+        def product(lhs_codes, lhs_scales, rhs_codes, rhs_scales, t, rhs_cols=slice(0, N), tag="bank"):
+            bank = psum.tile([P, N], F32, name="bank", tag=tag)
             cols = slice(t * P, (t + 1) * P)
             acc = bank[:, : rhs_cols.stop - rhs_cols.start]
             nc.tensor.matmul_mx(
@@ -93,26 +93,26 @@ def tile_picked_mombbondtrimlap_none_p_kernel(
 
         scale_table = keep.tile([P, T], U8, name="scale_table")
         nc.gpsimd.memset(scale_table[:].bitcast(I32), 0)
+        gate_rows = keep.tile([P, P], F32, name="gate_rows")
+        nc.gpsimd.memset(gate_rows[:], 0.0)
         two_l = load_list(two, "two_l")
+        offs_l = load_list(offs, "offs_l")
         word_table = keep.tile([P, T], I32, name="word_table")
         nc.sync.dma_start(word_table[:], x_words[0].rearrange("p n j -> p (n j)").bitcast(I32))
-        offs_l = load_list(offs, "offs_l")
         for q in range(4):
             nc.sync.dma_start(
                 scale_table[32 * q : 32 * q + 4, :].bitcast(I32), x_scales[0][4 * q : 4 * q + 4, :].bitcast(I32)
             )
         wb_raw = [load_weight_half(wb, h, "wb_raw%d" % h) for h in range(2)]
-        n3_l = load_list(n3, "n3_l")
-        n4_l = load_list(n4, "n4_l")
-        n5_l = load_list(n5, "n5_l")
-        wa_raw = [load_weight_half(wa, h, "wa_raw%d" % h) for h in range(2)]
-        gate_rows = keep.tile([P, P], F32, name="gate_rows")
-        nc.gpsimd.memset(gate_rows[:], 0.0)
         for first, g in ((0, gt), (PACK, gi)):
             nc.sync.dma_start(
                 gate_rows[first : first + PACK, :].rearrange("t (q r) -> t q r", r=8),
                 g.rearrange("(q t r) o -> t q (r o)", t=PACK, r=8),
             )
+        n4_l = load_list(n4, "n4_l")
+        n5_l = load_list(n5, "n5_l")
+        n3_l = load_list(n3, "n3_l")
+        wa_raw = [load_weight_half(wa, h, "wa_raw%d" % h) for h in range(2)]
         n1_l = load_list(n1, "n1_l")
         n2_l = load_list(n2, "n2_l")
         n6_l = load_list(n6, "n6_l")
@@ -131,59 +131,90 @@ def tile_picked_mombbondtrimlap_none_p_kernel(
         two_scales = deal_scales(two_sp, "two_s")
         wb_codes = keep.tile([P, N], U32, name="wb_codes", align_bytes=64)
         wb_scales = keep.tile([P, N], U8, name="wb_scales", align_bytes=64)
-        b_plain = [keep.tile([P, N], F32, name="b_plain%d" % t) for t in range(PACK)]
-        wb_bf = [round_weight_half(wb_raw[h], "wb_bf%d" % h) for h in range(2)]
+        wb_bf = [keep.tile([P, HALF, PACK], BF16, name="wb_bf%d" % h, tag="wb_bf%d" % h, align_bytes=64) for h in range(2)]
+        for h in range(2):
+            round_weight_half(wb_raw[h], wb_bf[h][:])
+
+        gate_bank = psum.tile([P, N], F32, name="bank")
+        nc.tensor.transpose(gate_bank[:, :P], gate_rows[:], ident[:])
+        gt_col, gi_col = gate_bank[:, :PACK], gate_bank[:, PACK : 2 * PACK]
+        abs_gi = keep.tile([P, PACK], F32, name="abs_gi")
+        neg_abs_gi = keep.tile([P, PACK], F32, name="neg_abs_gi", tag="after_b", align_bytes=64)
+        nc.scalar.activation(abs_gi[:], gi_col, ABS)
+        nc.scalar.activation(neg_abs_gi[:], abs_gi[:], COPY, scale=-1.0)
+        flip = keep.tile([P, PACK], F32, name="flip")
+        signed_gt = keep.tile([P, PACK], F32, name="signed_gt")
+        nc.vector.tensor_scalar(flip[:], gi_col, 0.0, -2.0, IS_GE, MULT)
+        nc.vector.scalar_tensor_tensor(signed_gt[:], flip[:], 1.0, gt_col, ADD, MULT)
+
         for h in range(2):
             quantise(wb_codes[:, halves[h]], wb_scales[:, halves[h]], wb_bf[h][:].rearrange("p c j -> p (c j)"))
             acc = product(two_words, two_scales, wb_codes, wb_scales, 0, halves[h])
-            nc.scalar.copy(windows[0][:, halves[h]], acc)
-            nc.scalar.copy(b_plain[0][:, halves[h]], acc)
+            nc.scalar.activation(windows[0][:, halves[h]], acc, COPY, scale=neg_abs_gi[:, 0:1])
         offs_sp = pick_scales(offs_l, "offs_s", "wb_bf1")
         offs_scales = deal_scales(offs_sp, "offs_s")
         for t in range(1, PACK):
             acc = product(two_words, two_scales, wb_codes, wb_scales, t)
-            nc.scalar.copy(windows[t][:, :N], acc)
-            nc.scalar.copy(b_plain[t][:], acc)
+            nc.scalar.activation(windows[t][:, :N], acc, COPY, scale=neg_abs_gi[:, t : t + 1])
 
-        gate_bank = psum.tile([P, N], F32, name="bank")
-        nc.tensor.transpose(gate_bank[:, :P], gate_rows[:], ident[:])
-        gt_col = keep.tile([P, PACK], F32, name="gt_col")
-        neg_gi_col = keep.tile([P, PACK], F32, name="neg_gi_col")
-        nc.scalar.copy(gt_col[:], gate_bank[:, :PACK])
-        nc.scalar.activation(neg_gi_col[:], gate_bank[:, PACK : 2 * PACK], COPY, scale=-1.0)
+        wa_bf = keep.tile([P, H, PACK], BF16, name="wa_bf", tag="after_b", align_bytes=64)
+        for h in range(2):
+            round_weight_half(wa_raw[h], wa_bf[:, halves[h], :])
 
-        wa_bf = [round_weight_half(wa_raw[h], "wa_bf%d" % h) for h in range(2)]
-
-        z2_bf = keep.tile([P, N, PACK], BF16, name="z2_bf", align_bytes=64)
+        sums = [psum.tile([P, PACK, P], F32, name="sums") for blk in range(PACK)]
         for pair in ((0, 1), (2, 3)):
-            u, v, w, m = {}, {}, {}, {}
+            g4 = {}
             for t in pair:
-                u[t] = ring.tile([P, N], F32, name="u")
-                nc.vector.tensor_tensor(u[t][:], windows[t][:].indirect(n3_l[:]), b_plain[t][:], ADD)
+                g4[t] = ring.tile([P, N], F32, name="g4")
+                nc.vector.tensor_copy(g4[t][:], windows[t][:].indirect(n4_l[:]))
             for t in pair:
-                v[t] = ring.tile([P, N], F32, name="v")
-                nc.vector.tensor_tensor(v[t][:], windows[t][:].indirect(n4_l[:]), u[t][:], SUB)
-            for t in pair:
-                w[t] = ring.tile([P, N], F32, name="w")
-                nc.vector.tensor_tensor(w[t][:], windows[t][:].indirect(n5_l[:]), u[t][:], SUB)
-            for t in pair:
-                m[t] = ring.tile([P, N], F32, name="m")
-                nc.vector.tensor_tensor(m[t][:], v[t][:], w[t][:], MAX)
-                nc.scalar.activation(z2_bf[:, :, t], m[t][:], COPY, scale=neg_gi_col[:, t : t + 1])
+                d = ring.tile([P, N], F32, name="d")
+                nc.vector.tensor_tensor(d[:], windows[t][:].indirect(n5_l[:]), g4[t][:], SUB)
+                rest = ring.tile([P, N], F32, name="rest")
+                nc.vector.tensor_tensor(rest[:], windows[t][:].indirect(n3_l[:]), g4[t][:], SUB)
+                excess = ring.tile([P, N], F32, name="excess")
+                nc.scalar.activation(excess[:], d[:], RELU, scale=-1.0)
+                terms = (windows[t], excess, rest)
+                for blk in range(PACK):
+                    for i, term in enumerate(terms):
+                        nc.tensor.matmul(
+                            sums[blk][:, t, :],
+                            lhsT=term[:, blk * P : (blk + 1) * P],
+                            rhs=ident[:],
+                            is_transpose=True,
+                            start=(i == 0),
+                            stop=(i == len(terms) - 1),
+                        )
             if pair[0] == 0:
                 wa_codes = keep.tile([P, H], U32, name="wa_codes", align_bytes=64)
                 wa_scales = keep.tile([P, H], U8, name="wa_scales", align_bytes=64)
-                for h in range(2):
-                    cols = slice(h * HALF, (h + 1) * HALF)
-                    quantise(wa_codes[:, cols], wa_scales[:, cols], wa_bf[h][:].rearrange("p c j -> p (c j)"))
+                quantise(wa_codes[:], wa_scales[:], wa_bf[:].rearrange("p c j -> p (c j)"))
                 a_rows = []
                 for t in range(PACK):
-                    bank = product(offs_words, offs_scales, wa_codes, wa_scales, t)
+                    acc = product(offs_words, offs_scales, wa_codes, wa_scales, t)
                     rows = keep.tile([P, H], F32, name="a_rows%d" % t)
-                    nc.scalar.copy(rows[:], bank)
+                    nc.scalar.copy(rows[:], acc)
                     a_rows.append(rows)
 
-        z_bf = [keep.tile([P, P, PACK], BF16, name="z_bf%d" % e, align_bytes=64) for e in range(PACK)]
+        z2_bf = keep.tile([P, N, PACK], BF16, name="z2_bf", align_bytes=64)
+        z2_words = z2_bf[:].rearrange("p c j -> p (c j)").bitcast(F32)
+        for h in range(2):
+            back = psum.tile([P, N], F32, name="bank")
+            for b in range(2):
+                blk = 2 * h + b
+                turned = keep.tile([P, 2, P, 2], BF16, name="turned", tag="turned%d" % blk, align_bytes=64)
+                nc.scalar.copy(turned[:], sums[blk][:].rearrange("c (u e) p -> c u p e", e=2))
+                words = turned[:].rearrange("c u p e -> c (u p e)").bitcast(F32)
+                for u in range(2):
+                    nc.tensor.transpose(
+                        back[:, (2 * b + u) * P : (2 * b + u + 1) * P], words[:, u * P : (u + 1) * P], ident[:]
+                    )
+            nc.scalar.copy(
+                z2_words[:, h * N : (h + 1) * N].rearrange("p (b c u) -> p b c u", b=2, u=2),
+                back[:].rearrange("p (b u c) -> p b c u", b=2, u=2),
+            )
+
+        z_bf = [keep.tile([P, P, PACK], BF16, name="z_bf%d" % e, tag="turned%d" % e, align_bytes=64) for e in range(PACK)]
         for pair in ((0, 1), (2, 3)):
             pa, pb, dt = {}, {}, {}
             for t in pair:
@@ -201,7 +232,7 @@ def tile_picked_mombbondtrimlap_none_p_kernel(
                 nc.vector.tensor_tensor(dt[t][:].indirect(n2_l[:]), pa[t][:], pb[t][:], MULT)
                 by_residue = dt[t][:].rearrange("p (m e) -> p e m", e=PACK)
                 for e in range(PACK):
-                    nc.scalar.activation(z_bf[e][:, :, t], by_residue[:, e, :], COPY, scale=gt_col[:, t : t + 1])
+                    nc.scalar.activation(z_bf[e][:, :, t], by_residue[:, e, :], COPY, scale=signed_gt[:, t : t + 1])
 
         z2_codes = keep.tile([P, N], U32, name="z2_codes", tag="late", align_bytes=64)
         z2_scales = keep.tile([P, N], U8, name="z2_scales", align_bytes=64)
@@ -220,7 +251,7 @@ def tile_picked_mombbondtrimlap_none_p_kernel(
                 nc.vector.tensor_scalar_mul(windows[e][:, halves[1]], right, 0.75 * 0.0625)
                 nc.vector.tensor_scalar_mul(neg_cv[e][:, halves[1]], right, -0.0625)
             else:
-                acc = product(z_codes, z_scales, z2_codes, z2_scales, e)
+                acc = product(z_codes, z_scales, z2_codes, z2_scales, e, tag="sums")
                 nc.scalar.activation(windows[e][:, :N], acc, COPY, scale=0.75 * 0.0625)
                 nc.scalar.activation(neg_cv[e][:], acc, COPY, scale=-0.0625)
 

@@ -16,9 +16,9 @@ FP8X4 = mybir.dt.float8_e4m3fn_x4
 ADD = mybir.AluOpType.add
 SUB = mybir.AluOpType.subtract
 MULT = mybir.AluOpType.mult
-IS_GE = mybir.AluOpType.is_ge
 COPY = mybir.ActivationFunctionType.Copy
 ABS = mybir.ActivationFunctionType.Abs
+SIGN = mybir.ActivationFunctionType.Sign
 RELU = mybir.ActivationFunctionType.Relu
 
 P = 128
@@ -96,14 +96,14 @@ def tile_picked_mombbondtrimlap_none_p_kernel(
         gate_rows = keep.tile([P, P], F32, name="gate_rows")
         nc.gpsimd.memset(gate_rows[:], 0.0)
         two_l = load_list(two, "two_l")
-        offs_l = load_list(offs, "offs_l")
-        word_table = keep.tile([P, T], I32, name="word_table")
-        nc.sync.dma_start(word_table[:], x_words[0].rearrange("p n j -> p (n j)").bitcast(I32))
         for q in range(4):
             nc.sync.dma_start(
                 scale_table[32 * q : 32 * q + 4, :].bitcast(I32), x_scales[0][4 * q : 4 * q + 4, :].bitcast(I32)
             )
+        offs_l = load_list(offs, "offs_l")
         wb_raw = [load_weight_half(wb, h, "wb_raw%d" % h) for h in range(2)]
+        word_table = keep.tile([P, T], I32, name="word_table")
+        nc.sync.dma_start(word_table[:], x_words[0].rearrange("p n j -> p (n j)").bitcast(I32))
         for first, g in ((0, gt), (PACK, gi)):
             nc.sync.dma_start(
                 gate_rows[first : first + PACK, :].rearrange("t (q r) -> t q r", r=8),
@@ -125,37 +125,39 @@ def tile_picked_mombbondtrimlap_none_p_kernel(
             nc.vector.memset(windows[t][:, N:], 0.0)
 
         halves = [slice(h * HALF, (h + 1) * HALF) for h in range(2)]
-        two_words = pick_words(two_l, "two_w")
-        offs_words = pick_words(offs_l, "offs_w")
         two_sp = pick_scales(two_l, "two_s", "two_s_picked")
+        offs_sp = pick_scales(offs_l, "offs_s", "offs_s_picked")
         two_scales = deal_scales(two_sp, "two_s")
+        offs_scales = deal_scales(offs_sp, "offs_s")
         wb_codes = keep.tile([P, N], U32, name="wb_codes", align_bytes=64)
         wb_scales = keep.tile([P, N], U8, name="wb_scales", align_bytes=64)
-        wb_bf = [keep.tile([P, HALF, PACK], BF16, name="wb_bf%d" % h, tag="wb_bf%d" % h, align_bytes=64) for h in range(2)]
+        wb_bf = keep.tile([P, N, PACK], BF16, name="wb_bf", align_bytes=64)
         for h in range(2):
-            round_weight_half(wb_raw[h], wb_bf[h][:])
+            round_weight_half(wb_raw[h], wb_bf[:, halves[h], :])
+        quantise(wb_codes[:], wb_scales[:], wb_bf[:].rearrange("p c j -> p (c j)"))
+        two_words = pick_words(two_l, "two_w")
+        offs_words = pick_words(offs_l, "offs_w")
 
         gate_bank = psum.tile([P, N], F32, name="bank")
         nc.tensor.transpose(gate_bank[:, :P], gate_rows[:], ident[:])
-        gt_col, gi_col = gate_bank[:, :PACK], gate_bank[:, PACK : 2 * PACK]
         abs_gi = keep.tile([P, PACK], F32, name="abs_gi")
         neg_abs_gi = keep.tile([P, PACK], F32, name="neg_abs_gi", tag="after_b", align_bytes=64)
-        nc.scalar.activation(abs_gi[:], gi_col, ABS)
+        nc.scalar.activation(abs_gi[:], gate_bank[:, PACK : 2 * PACK], ABS)
         nc.scalar.activation(neg_abs_gi[:], abs_gi[:], COPY, scale=-1.0)
-        flip = keep.tile([P, PACK], F32, name="flip")
-        signed_gt = keep.tile([P, PACK], F32, name="signed_gt")
-        nc.vector.tensor_scalar(flip[:], gi_col, 0.0, -2.0, IS_GE, MULT)
-        nc.vector.scalar_tensor_tensor(signed_gt[:], flip[:], 1.0, gt_col, ADD, MULT)
+        gates = keep.tile([P, 2 * PACK], F32, name="gates")
+        nc.scalar.copy(gates[:], gate_bank[:, : 2 * PACK])
 
-        for h in range(2):
-            quantise(wb_codes[:, halves[h]], wb_scales[:, halves[h]], wb_bf[h][:].rearrange("p c j -> p (c j)"))
-            acc = product(two_words, two_scales, wb_codes, wb_scales, 0, halves[h])
-            nc.scalar.activation(windows[0][:, halves[h]], acc, COPY, scale=neg_abs_gi[:, 0:1])
-        offs_sp = pick_scales(offs_l, "offs_s", "wb_bf1")
-        offs_scales = deal_scales(offs_sp, "offs_s")
-        for t in range(1, PACK):
+        for t in range(PACK):
             acc = product(two_words, two_scales, wb_codes, wb_scales, t)
             nc.scalar.activation(windows[t][:, :N], acc, COPY, scale=neg_abs_gi[:, t : t + 1])
+
+        sign_gi = keep.tile([P, PACK], F32, name="sign_gi", tag="after_b", align_bytes=64)
+        flip = keep.tile([P, PACK], F32, name="flip")
+        signed_gt = keep.tile([P, PACK], F32, name="signed_gt")
+        nc.scalar.activation(sign_gi[:], gates[:, PACK:], SIGN)
+        nc.scalar.activation(flip[:], sign_gi[:], SIGN, scale=-1.0, bias=-0.5)
+        for t in range(PACK):
+            nc.scalar.activation(signed_gt[:, t : t + 1], gates[:, t : t + 1], COPY, scale=flip[:, t : t + 1])
 
         wa_bf = keep.tile([P, H, PACK], BF16, name="wa_bf", tag="after_b", align_bytes=64)
         for h in range(2):
@@ -168,12 +170,15 @@ def tile_picked_mombbondtrimlap_none_p_kernel(
                 g4[t] = ring.tile([P, N], F32, name="g4")
                 nc.vector.tensor_copy(g4[t][:], windows[t][:].indirect(n4_l[:]))
             for t in pair:
-                d = ring.tile([P, N], F32, name="d")
-                nc.vector.tensor_tensor(d[:], windows[t][:].indirect(n5_l[:]), g4[t][:], SUB)
-                rest = ring.tile([P, N], F32, name="rest")
-                nc.vector.tensor_tensor(rest[:], windows[t][:].indirect(n3_l[:]), g4[t][:], SUB)
+                if t == PACK - 1:
+                    both = keep.tile([P, 2, N], F32, name="both_last", tag="after_b", align_bytes=64)
+                else:
+                    both = ring.tile([P, 2, N], F32, name="both", bufs=3)
+                d, rest = both[:, 0, :], both[:, 1, :]
+                nc.vector.tensor_tensor(d, windows[t][:].indirect(n5_l[:]), g4[t][:], SUB)
+                nc.vector.tensor_tensor(rest, windows[t][:].indirect(n3_l[:]), g4[t][:], SUB)
                 excess = ring.tile([P, N], F32, name="excess")
-                nc.scalar.activation(excess[:], d[:], RELU, scale=-1.0)
+                nc.scalar.activation(excess[:], d, RELU, scale=-1.0)
                 terms = (windows[t], excess, rest)
                 for blk in range(PACK):
                     for i, term in enumerate(terms):

@@ -23,8 +23,16 @@ RELU = mybir.ActivationFunctionType.Relu
 
 P = 128
 PACK = 4
+BLOCK_PARTS = 8
+QUADRANT = 32
+PER_COLUMN = 16
 WIDE = 1024
 HALF = 256
+LINE = 4
+CV_SCALE = 0.0625
+PAIR_SCALE = 0.75
+PAIRS = ((0, 1), (2, 3))
+LAST = PACK - 1
 
 
 def tile_picked_mombbondtrimlap_none_p_kernel(
@@ -34,56 +42,56 @@ def tile_picked_mombbondtrimlap_none_p_kernel(
     with ExitStack() as ctx:
         keep = ctx.enter_context(tc.tile_pool(name="keep", bufs=1))
         ring = ctx.enter_context(tc.tile_pool(name="ring", bufs=2))
-        psum = ctx.enter_context(tc.psum_pool(name="psum", bufs=4))
+        psum = ctx.enter_context(tc.psum_pool(name="psum", bufs=PACK))
 
         def load_list(src, name):
             tile = keep.tile(list(src.shape), U16, name=name)
             nc.sync.dma_start(tile[:], src)
             return tile
 
-        def load_weight_half(w, half, name):
-            raw = keep.tile([P, PACK, HALF], F32, name=name)
-            nc.sync.dma_start(raw[:], w.rearrange("(p j) n -> p j n", j=PACK)[:, :, half * HALF : (half + 1) * HALF])
+        def load_weight(w, cols, name):
+            raw = keep.tile([P, PACK, cols.stop - cols.start], F32, name=name)
+            nc.sync.dma_start(raw[:], w.rearrange("(p j) n -> p j n", j=PACK)[:, :, cols])
             return raw
 
-        def round_weight_half(raw, grouped):
+        def round_weight(raw, grouped):
             nc.scalar.copy(
-                grouped.rearrange("p (c i) j -> p c j i", i=4),
-                raw[:].rearrange("p j (c i) -> p c j i", i=4),
+                grouped.rearrange("p (c i) j -> p c j i", i=LINE),
+                raw.rearrange("p j (c i) -> p c j i", i=LINE),
             )
 
         def quantise(codes, scales, grouped):
-            nc.vector.quantize_mx(out=codes.bitcast(FP8X4), scales=scales, in_=grouped)
+            nc.vector.quantize_mx(out=codes.bitcast(FP8X4), scales=scales, in_=grouped.rearrange("p c j -> p (c j)"))
 
-        def pick_scales(lst, name, tag):
-            picked = keep.tile([P, S], U8, name=name + "_picked", tag=tag, align_bytes=64)
-            nc.vector.tensor_copy(picked[:], scale_table[:].indirect(lst[:]))
+        def pick_scales(picks, name):
+            picked = keep.tile([P, S], U8, name=name, align_bytes=64)
+            nc.vector.tensor_copy(picked[:], scale_table[:].indirect(picks[:]))
             return picked
 
         def deal_scales(picked, name):
-            dealt = keep.tile([P, S], U8, name=name + "_dealt", align_bytes=64)
+            dealt = keep.tile([P, S], U8, name=name, align_bytes=64)
             nc.vector.tensor_copy(
-                dealt[:].bitcast(I32).rearrange("p (t q w) -> p t q w", t=PACK, w=2),
-                picked[:].bitcast(I32).rearrange("p (q t w) -> p t q w", t=PACK, w=2),
+                dealt[:].bitcast(I32).rearrange("p (t q w) -> p t q w", t=PACK, w=BLOCK_PARTS // 4),
+                picked[:].bitcast(I32).rearrange("p (q t w) -> p t q w", t=PACK, w=BLOCK_PARTS // 4),
             )
             return dealt
 
-        def pick_words(lst, name):
-            picked = keep.tile([P, S], U32, name=name, align_bytes=64)
+        def pick_words(picks, name, tag):
+            picked = keep.tile([P, S], U32, name=name, tag=tag, align_bytes=64)
             nc.vector.tensor_copy(
-                picked[:].rearrange("p (t q r) -> p q t r", t=PACK, r=8),
-                word_table[:].bitcast(U32).indirect(lst[:]),
+                picked[:].rearrange("p (t q r) -> p q t r", t=PACK, r=BLOCK_PARTS),
+                word_table[:].bitcast(U32).indirect(picks[:]),
             )
             return picked
 
-        def product(lhs_codes, lhs_scales, rhs_codes, rhs_scales, t, rhs_cols=slice(0, N), tag="bank"):
+        def product(lhs_codes, lhs_scales, rhs_codes, rhs_scales, row_tile, rhs_cols=slice(0, N), tag="bank"):
             bank = psum.tile([P, N], F32, name="bank", tag=tag)
-            cols = slice(t * P, (t + 1) * P)
+            lhs_cols = slice(row_tile * P, (row_tile + 1) * P)
             acc = bank[:, : rhs_cols.stop - rhs_cols.start]
             nc.tensor.matmul_mx(
                 out=acc,
-                lhsT=lhs_codes[:, cols].bitcast(FP8X4),
-                lhsT_scale=lhs_scales[:, cols],
+                lhsT=lhs_codes[:, lhs_cols].bitcast(FP8X4),
+                lhsT_scale=lhs_scales[:, lhs_cols],
                 rhs=rhs_codes[:, rhs_cols].bitcast(FP8X4),
                 rhs_scale=rhs_scales[:, rhs_cols],
                 start=True,
@@ -91,32 +99,36 @@ def tile_picked_mombbondtrimlap_none_p_kernel(
             )
             return acc
 
+        halves = [slice(half * HALF, (half + 1) * HALF) for half in range(2)]
+
         scale_table = keep.tile([P, T], U8, name="scale_table")
         nc.gpsimd.memset(scale_table[:].bitcast(I32), 0)
         gate_rows = keep.tile([P, P], F32, name="gate_rows")
         nc.gpsimd.memset(gate_rows[:], 0.0)
-        two_l = load_list(two, "two_l")
-        for q in range(4):
+        two_list = load_list(two, "two_list")
+        offs_list = load_list(offs, "offs_list")
+        wb_raw = [load_weight(wb, halves[0], "wb_raw0")]
+        for quad in range(P // QUADRANT):
             nc.sync.dma_start(
-                scale_table[32 * q : 32 * q + 4, :].bitcast(I32), x_scales[0][4 * q : 4 * q + 4, :].bitcast(I32)
+                scale_table[QUADRANT * quad : QUADRANT * quad + 4, :].bitcast(I32),
+                x_scales[0][4 * quad : 4 * quad + 4, :].bitcast(I32),
             )
-        offs_l = load_list(offs, "offs_l")
-        wb_raw = [load_weight_half(wb, h, "wb_raw%d" % h) for h in range(2)]
         word_table = keep.tile([P, T], I32, name="word_table")
         nc.sync.dma_start(word_table[:], x_words[0].rearrange("p n j -> p (n j)").bitcast(I32))
-        for first, g in ((0, gt), (PACK, gi)):
+        wb_raw.append(load_weight(wb, halves[1], "wb_raw1"))
+        for first, gate in ((0, gt), (PACK, gi)):
             nc.sync.dma_start(
-                gate_rows[first : first + PACK, :].rearrange("t (q r) -> t q r", r=8),
-                g.rearrange("(q t r) o -> t q (r o)", t=PACK, r=8),
+                gate_rows[first : first + PACK, :].rearrange("t (q r) -> t q r", r=BLOCK_PARTS),
+                gate.rearrange("(q t r) o -> t q (r o)", t=PACK, r=BLOCK_PARTS),
             )
-        n4_l = load_list(n4, "n4_l")
-        n5_l = load_list(n5, "n5_l")
-        n3_l = load_list(n3, "n3_l")
-        wa_raw = [load_weight_half(wa, h, "wa_raw%d" % h) for h in range(2)]
-        n1_l = load_list(n1, "n1_l")
-        n2_l = load_list(n2, "n2_l")
-        n6_l = load_list(n6, "n6_l")
-        n7_l = load_list(n7, "n7_l")
+        n4_list = load_list(n4, "n4_list")
+        n5_list = load_list(n5, "n5_list")
+        n3_list = load_list(n3, "n3_list")
+        wa_raw = load_weight(wa, slice(0, H), "wa_raw")
+        n1_list = load_list(n1, "n1_list")
+        n2_list = load_list(n2, "n2_list")
+        n6_list = load_list(n6, "n6_list")
+        n7_list = load_list(n7, "n7_list")
         ident = keep.tile([P, P], F32, name="ident")
         make_identity(nc, ident[:])
 
@@ -124,34 +136,39 @@ def tile_picked_mombbondtrimlap_none_p_kernel(
         for t in range(PACK):
             nc.vector.memset(windows[t][:, N:], 0.0)
 
-        halves = [slice(h * HALF, (h + 1) * HALF) for h in range(2)]
-        two_sp = pick_scales(two_l, "two_s", "two_s_picked")
-        offs_sp = pick_scales(offs_l, "offs_s", "offs_s_picked")
-        two_scales = deal_scales(two_sp, "two_s")
-        offs_scales = deal_scales(offs_sp, "offs_s")
+        two_picked = pick_scales(two_list, "two_picked")
+        offs_picked = pick_scales(offs_list, "offs_picked")
+        two_scales = deal_scales(two_picked, "two_scales")
+        offs_scales = deal_scales(offs_picked, "offs_scales")
         wb_codes = keep.tile([P, N], U32, name="wb_codes", align_bytes=64)
         wb_scales = keep.tile([P, N], U8, name="wb_scales", align_bytes=64)
-        wb_bf = keep.tile([P, N, PACK], BF16, name="wb_bf", align_bytes=64)
-        for h in range(2):
-            round_weight_half(wb_raw[h], wb_bf[:, halves[h], :])
-        quantise(wb_codes[:], wb_scales[:], wb_bf[:].rearrange("p c j -> p (c j)"))
-        two_words = pick_words(two_l, "two_w")
-        offs_words = pick_words(offs_l, "offs_w")
+        wb_bf = [
+            keep.tile([P, HALF, PACK], BF16, name="wb_bf%d" % half, tag="wb_bf%d" % half, align_bytes=64)
+            for half in range(2)
+        ]
+        for half in range(2):
+            round_weight(wb_raw[half][:], wb_bf[half][:])
+        two_words = pick_words(two_list, "two_words", "two_words")
 
         gate_bank = psum.tile([P, N], F32, name="bank")
         nc.tensor.transpose(gate_bank[:, :P], gate_rows[:], ident[:])
         abs_gi = keep.tile([P, PACK], F32, name="abs_gi")
-        neg_abs_gi = keep.tile([P, PACK], F32, name="neg_abs_gi", tag="after_b", align_bytes=64)
+        neg_abs_gi = keep.tile([P, PACK], F32, name="neg_abs_gi", tag="after_nb", align_bytes=64)
         nc.scalar.activation(abs_gi[:], gate_bank[:, PACK : 2 * PACK], ABS)
         nc.scalar.activation(neg_abs_gi[:], abs_gi[:], COPY, scale=-1.0)
         gates = keep.tile([P, 2 * PACK], F32, name="gates")
         nc.scalar.copy(gates[:], gate_bank[:, : 2 * PACK])
 
-        for t in range(PACK):
+        for half in range(2):
+            quantise(wb_codes[:, halves[half]], wb_scales[:, halves[half]], wb_bf[half][:])
+            acc = product(two_words, two_scales, wb_codes, wb_scales, 0, halves[half])
+            nc.scalar.activation(windows[0][:, halves[half]], acc, COPY, scale=neg_abs_gi[:, 0:1])
+        offs_words = pick_words(offs_list, "offs_words", "wb_bf1")
+        for t in range(1, PACK):
             acc = product(two_words, two_scales, wb_codes, wb_scales, t)
             nc.scalar.activation(windows[t][:, :N], acc, COPY, scale=neg_abs_gi[:, t : t + 1])
 
-        sign_gi = keep.tile([P, PACK], F32, name="sign_gi", tag="after_b", align_bytes=64)
+        sign_gi = keep.tile([P, PACK], F32, name="sign_gi", tag="after_nb", align_bytes=64)
         flip = keep.tile([P, PACK], F32, name="flip")
         signed_gt = keep.tile([P, PACK], F32, name="signed_gt")
         nc.scalar.activation(sign_gi[:], gates[:, PACK:], SIGN)
@@ -159,41 +176,41 @@ def tile_picked_mombbondtrimlap_none_p_kernel(
         for t in range(PACK):
             nc.scalar.activation(signed_gt[:, t : t + 1], gates[:, t : t + 1], COPY, scale=flip[:, t : t + 1])
 
-        wa_bf = keep.tile([P, H, PACK], BF16, name="wa_bf", tag="after_b", align_bytes=64)
-        for h in range(2):
-            round_weight_half(wa_raw[h], wa_bf[:, halves[h], :])
+        wa_bf = keep.tile([P, H, PACK], BF16, name="wa_bf", tag="after_nb", align_bytes=64)
+        for half in range(2):
+            round_weight(wa_raw[:, :, halves[half]], wa_bf[:, halves[half], :])
 
         sums = [psum.tile([P, PACK, P], F32, name="sums") for blk in range(PACK)]
-        for pair in ((0, 1), (2, 3)):
-            g4 = {}
+        for pair in PAIRS:
+            at_n4 = {}
             for t in pair:
-                g4[t] = ring.tile([P, N], F32, name="g4")
-                nc.vector.tensor_copy(g4[t][:], windows[t][:].indirect(n4_l[:]))
+                at_n4[t] = ring.tile([P, N], F32, name="at_n4")
+                nc.vector.tensor_copy(at_n4[t][:], windows[t][:].indirect(n4_list[:]))
             for t in pair:
-                if t == PACK - 1:
-                    both = keep.tile([P, 2, N], F32, name="both_last", tag="after_b", align_bytes=64)
+                if t == LAST:
+                    both = keep.tile([P, 2, N], F32, name="both_last", tag="after_nb", align_bytes=64)
                 else:
-                    both = ring.tile([P, 2, N], F32, name="both", bufs=3)
-                d, rest = both[:, 0, :], both[:, 1, :]
-                nc.vector.tensor_tensor(d, windows[t][:].indirect(n5_l[:]), g4[t][:], SUB)
-                nc.vector.tensor_tensor(rest, windows[t][:].indirect(n3_l[:]), g4[t][:], SUB)
+                    both = ring.tile([P, 2, N], F32, name="both", bufs=LAST)
+                diff, rest = both[:, 0, :], both[:, 1, :]
+                nc.vector.tensor_tensor(diff, windows[t][:].indirect(n5_list[:]), at_n4[t][:], SUB)
+                nc.vector.tensor_tensor(rest, windows[t][:].indirect(n3_list[:]), at_n4[t][:], SUB)
                 excess = ring.tile([P, N], F32, name="excess")
-                nc.scalar.activation(excess[:], d, RELU, scale=-1.0)
+                nc.scalar.activation(excess[:], diff, RELU, scale=-1.0)
                 terms = (windows[t], excess, rest)
                 for blk in range(PACK):
-                    for i, term in enumerate(terms):
+                    for place, term in enumerate(terms):
                         nc.tensor.matmul(
                             sums[blk][:, t, :],
                             lhsT=term[:, blk * P : (blk + 1) * P],
                             rhs=ident[:],
                             is_transpose=True,
-                            start=(i == 0),
-                            stop=(i == len(terms) - 1),
+                            start=(place == 0),
+                            stop=(place == len(terms) - 1),
                         )
-            if pair[0] == 0:
+            if pair == PAIRS[0]:
                 wa_codes = keep.tile([P, H], U32, name="wa_codes", align_bytes=64)
                 wa_scales = keep.tile([P, H], U8, name="wa_scales", align_bytes=64)
-                quantise(wa_codes[:], wa_scales[:], wa_bf[:].rearrange("p c j -> p (c j)"))
+                quantise(wa_codes[:], wa_scales[:], wa_bf[:])
                 a_rows = []
                 for t in range(PACK):
                     acc = product(offs_words, offs_scales, wa_codes, wa_scales, t)
@@ -202,74 +219,75 @@ def tile_picked_mombbondtrimlap_none_p_kernel(
                     a_rows.append(rows)
 
         z2_bf = keep.tile([P, N, PACK], BF16, name="z2_bf", align_bytes=64)
-        z2_words = z2_bf[:].rearrange("p c j -> p (c j)").bitcast(F32)
-        for h in range(2):
+        z2_pairs = z2_bf[:].rearrange("p c t -> p (c t)").bitcast(F32)
+        for half in range(2):
             back = psum.tile([P, N], F32, name="bank")
-            for b in range(2):
-                blk = 2 * h + b
+            for sub in range(2):
+                blk = 2 * half + sub
                 turned = keep.tile([P, 2, P, 2], BF16, name="turned", tag="turned%d" % blk, align_bytes=64)
-                nc.scalar.copy(turned[:], sums[blk][:].rearrange("c (u e) p -> c u p e", e=2))
-                words = turned[:].rearrange("c u p e -> c (u p e)").bitcast(F32)
+                nc.scalar.copy(turned[:], sums[blk][:].rearrange("c (u v) p -> c u p v", v=2))
+                turned_pairs = turned[:].rearrange("c u p v -> c (u p v)").bitcast(F32)
                 for u in range(2):
                     nc.tensor.transpose(
-                        back[:, (2 * b + u) * P : (2 * b + u + 1) * P], words[:, u * P : (u + 1) * P], ident[:]
+                        back[:, (2 * sub + u) * P : (2 * sub + u + 1) * P], turned_pairs[:, u * P : (u + 1) * P], ident[:]
                     )
             nc.scalar.copy(
-                z2_words[:, h * N : (h + 1) * N].rearrange("p (b c u) -> p b c u", b=2, u=2),
+                z2_pairs[:, half * N : (half + 1) * N].rearrange("p (b c u) -> p b c u", b=2, u=2),
                 back[:].rearrange("p (b u c) -> p b c u", b=2, u=2),
             )
 
-        z_bf = [keep.tile([P, P, PACK], BF16, name="z_bf%d" % e, tag="turned%d" % e, align_bytes=64) for e in range(PACK)]
-        for pair in ((0, 1), (2, 3)):
+        z_bf = [
+            keep.tile([P, P, PACK], BF16, name="z_bf%d" % e, tag="turned%d" % e, align_bytes=64) for e in range(PACK)
+        ]
+        for pair in PAIRS:
             pa, pb, dt = {}, {}, {}
             for t in pair:
                 pa[t] = ring.tile([P, HALF], F32, name="pa")
-                nc.vector.tensor_copy(pa[t][:], a_rows[t][:].indirect(n1_l[:]))
-                if t == PACK - 1:
-                    pb[t] = keep.tile([P, HALF], F32, name="pb_last", tag="late", align_bytes=64)
+                nc.vector.tensor_copy(pa[t][:], a_rows[t][:].indirect(n1_list[:]))
+                if t == LAST:
+                    pb[t] = keep.tile([P, HALF], F32, name="pb_last", tag="after_scatter", align_bytes=64)
                 else:
                     pb[t] = ring.tile([P, HALF], F32, name="pb")
-                nc.vector.tensor_copy(pb[t][:], a_rows[t][:].indirect(n2_l[:]))
+                nc.vector.tensor_copy(pb[t][:], a_rows[t][:].indirect(n2_list[:]))
             for t in pair:
                 dt[t] = ring.tile([P, H], F32, name="dt")
-                nc.vector.tensor_tensor(dt[t][:].indirect(n1_l[:]), pa[t][:], pb[t][:], ADD)
+                nc.vector.tensor_tensor(dt[t][:].indirect(n1_list[:]), pa[t][:], pb[t][:], ADD)
             for t in pair:
-                nc.vector.tensor_tensor(dt[t][:].indirect(n2_l[:]), pa[t][:], pb[t][:], MULT)
+                nc.vector.tensor_tensor(dt[t][:].indirect(n2_list[:]), pa[t][:], pb[t][:], MULT)
                 by_residue = dt[t][:].rearrange("p (m e) -> p e m", e=PACK)
                 for e in range(PACK):
                     nc.scalar.activation(z_bf[e][:, :, t], by_residue[:, e, :], COPY, scale=signed_gt[:, t : t + 1])
 
-        z2_codes = keep.tile([P, N], U32, name="z2_codes", tag="late", align_bytes=64)
+        z2_codes = keep.tile([P, N], U32, name="z2_codes", tag="after_scatter", align_bytes=64)
         z2_scales = keep.tile([P, N], U8, name="z2_scales", align_bytes=64)
-        quantise(z2_codes[:], z2_scales[:], z2_bf[:].rearrange("p c j -> p (c j)"))
+        quantise(z2_codes[:], z2_scales[:], z2_bf[:])
         z_codes = keep.tile([P, H], U32, name="z_codes", align_bytes=64)
         z_scales = keep.tile([P, H], U8, name="z_scales", align_bytes=64)
         neg_cv = [keep.tile([P, N], F32, name="neg_cv%d" % e) for e in range(PACK)]
         for e in range(PACK):
-            cols = slice(e * P, (e + 1) * P)
-            quantise(z_codes[:, cols], z_scales[:, cols], z_bf[e][:].rearrange("p c j -> p (c j)"))
+            quantise(z_codes[:, e * P : (e + 1) * P], z_scales[:, e * P : (e + 1) * P], z_bf[e][:])
             if e == 0:
                 left = product(z_codes, z_scales, z2_codes, z2_scales, e, halves[0])
                 right = product(z_codes, z_scales, z2_codes, z2_scales, e, halves[1])
-                nc.scalar.activation(windows[e][:, halves[0]], left, COPY, scale=0.75 * 0.0625)
-                nc.scalar.activation(neg_cv[e][:, halves[0]], left, COPY, scale=-0.0625)
-                nc.vector.tensor_scalar_mul(windows[e][:, halves[1]], right, 0.75 * 0.0625)
-                nc.vector.tensor_scalar_mul(neg_cv[e][:, halves[1]], right, -0.0625)
+                nc.vector.tensor_scalar_mul(windows[e][:, halves[0]], left, PAIR_SCALE * CV_SCALE)
+                nc.vector.tensor_scalar_mul(neg_cv[e][:, halves[0]], left, -CV_SCALE)
+                nc.scalar.activation(windows[e][:, halves[1]], right, COPY, scale=PAIR_SCALE * CV_SCALE)
+                nc.scalar.activation(neg_cv[e][:, halves[1]], right, COPY, scale=-CV_SCALE)
             else:
                 acc = product(z_codes, z_scales, z2_codes, z2_scales, e, tag="sums")
-                nc.scalar.activation(windows[e][:, :N], acc, COPY, scale=0.75 * 0.0625)
-                nc.scalar.activation(neg_cv[e][:], acc, COPY, scale=-0.0625)
+                nc.scalar.activation(windows[e][:, :N], acc, COPY, scale=PAIR_SCALE * CV_SCALE)
+                nc.scalar.activation(neg_cv[e][:], acc, COPY, scale=-CV_SCALE)
 
-        out_rows = out.rearrange("(m e) n -> e m n", e=PACK)
-        for pair in ((0, 1), (2, 3)):
+        out_rows = out.rearrange("(p e) n -> e p n", e=PACK)
+        for pair in PAIRS:
             part = {}
             for e in pair:
                 part[e] = ring.tile([P, N], F32, name="part")
-                nc.vector.tensor_tensor(part[e][:], windows[e][:].indirect(n6_l[:]), neg_cv[e][:], ADD)
+                nc.vector.tensor_tensor(part[e][:], windows[e][:].indirect(n6_list[:]), neg_cv[e][:], ADD)
             for e in pair:
-                pieces = halves if e == PACK - 1 else [slice(0, N)]
+                pieces = halves if e == LAST else [slice(0, N)]
                 for cols in pieces:
                     res = ring.tile([P, cols.stop - cols.start], F32, name="res", bufs=3)
-                    entries = n7_l[:, cols.start // 16 : cols.stop // 16]
+                    entries = n7_list[:, cols.start // PER_COLUMN : cols.stop // PER_COLUMN]
                     nc.vector.tensor_tensor(res[:], windows[e][:].indirect(entries), part[e][:, cols], ADD)
                     nc.sync.dma_start(out_rows[e][:, cols], res[:])

from contextlib import ExitStack

import concourse.mybir as mybir
from concourse.masks import make_identity

K, T, S, N, H = 512, 2048, 512, 512, 512
FLOPS = 2 * K * S * H + 2 * K * S * N + 2 * S * H * N

F32 = mybir.dt.float32
BF16 = mybir.dt.bfloat16
I32 = mybir.dt.int32
U32 = mybir.dt.uint32
U16 = mybir.dt.uint16
U8 = mybir.dt.uint8
FP8X4 = mybir.dt.float8_e4m3fn_x4
ADD = mybir.AluOpType.add
SUB = mybir.AluOpType.subtract
MULT = mybir.AluOpType.mult
COPY = mybir.ActivationFunctionType.Copy
ABS = mybir.ActivationFunctionType.Abs
SIGN = mybir.ActivationFunctionType.Sign
RELU = mybir.ActivationFunctionType.Relu

P = 128
PACK = 4
BLOCK_PARTS = 8
QUADRANT = 32
PER_COLUMN = 16
WIDE = 1024
HALF = 256
LINE = 4
CV_SCALE = 0.0625
PAIR_SCALE = 0.75
PAIRS = ((0, 1), (2, 3))
LAST = PACK - 1


def tile_picked_mombbondtrimlap_none_p_kernel(
    tc, x_words, x_scales, wa, wb, gt, gi, offs, two, n1, n2, n3, n4, n5, n6, n7, out
):
    nc = tc.nc
    with ExitStack() as ctx:
        keep = ctx.enter_context(tc.tile_pool(name="keep", bufs=1))
        ring = ctx.enter_context(tc.tile_pool(name="ring", bufs=2))
        psum = ctx.enter_context(tc.psum_pool(name="psum", bufs=PACK))

        def load_list(src, name):
            tile = keep.tile(list(src.shape), U16, name=name)
            nc.sync.dma_start(tile[:], src)
            return tile

        def load_weight(w, cols, name):
            raw = keep.tile([P, PACK, cols.stop - cols.start], F32, name=name)
            nc.sync.dma_start(raw[:], w.rearrange("(p j) n -> p j n", j=PACK)[:, :, cols])
            return raw

        def round_weight(raw, grouped):
            nc.scalar.copy(
                grouped.rearrange("p (c i) j -> p c j i", i=LINE),
                raw.rearrange("p j (c i) -> p c j i", i=LINE),
            )

        def quantise(codes, scales, grouped):
            nc.vector.quantize_mx(out=codes.bitcast(FP8X4), scales=scales, in_=grouped.rearrange("p c j -> p (c j)"))

        def pick_scales(picks, name):
            picked = keep.tile([P, S], U8, name=name, align_bytes=64)
            nc.vector.tensor_copy(picked[:], scale_table[:].indirect(picks[:]))
            return picked

        def deal_scales(picked, name):
            dealt = keep.tile([P, S], U8, name=name, align_bytes=64)
            nc.vector.tensor_copy(
                dealt[:].bitcast(I32).rearrange("p (t q w) -> p t q w", t=PACK, w=BLOCK_PARTS // 4),
                picked[:].bitcast(I32).rearrange("p (q t w) -> p t q w", t=PACK, w=BLOCK_PARTS // 4),
            )
            return dealt

        def pick_words(picks, name, tag):
            picked = keep.tile([P, S], U32, name=name, tag=tag, align_bytes=64)
            nc.vector.tensor_copy(
                picked[:].rearrange("p (t q r) -> p q t r", t=PACK, r=BLOCK_PARTS),
                word_table[:].bitcast(U32).indirect(picks[:]),
            )
            return picked

        def product(lhs_codes, lhs_scales, rhs_codes, rhs_scales, row_tile, rhs_cols=slice(0, N), tag="bank"):
            bank = psum.tile([P, N], F32, name="bank", tag=tag)
            lhs_cols = slice(row_tile * P, (row_tile + 1) * P)
            acc = bank[:, : rhs_cols.stop - rhs_cols.start]
            nc.tensor.matmul_mx(
                out=acc,
                lhsT=lhs_codes[:, lhs_cols].bitcast(FP8X4),
                lhsT_scale=lhs_scales[:, lhs_cols],
                rhs=rhs_codes[:, rhs_cols].bitcast(FP8X4),
                rhs_scale=rhs_scales[:, rhs_cols],
                start=True,
                stop=True,
            )
            return acc

        halves = [slice(half * HALF, (half + 1) * HALF) for half in range(2)]

        scale_table = keep.tile([P, T], U8, name="scale_table")
        nc.gpsimd.memset(scale_table[:].bitcast(I32), 0)
        gate_rows = keep.tile([P, P], F32, name="gate_rows")
        nc.gpsimd.memset(gate_rows[:], 0.0)
        two_list = load_list(two, "two_list")
        offs_list = load_list(offs, "offs_list")
        wb_raw = [load_weight(wb, halves[0], "wb_raw0")]
        for quad in range(P // QUADRANT):
            nc.sync.dma_start(
                scale_table[QUADRANT * quad : QUADRANT * quad + 4, :].bitcast(I32),
                x_scales[0][4 * quad : 4 * quad + 4, :].bitcast(I32),
            )
        word_table = keep.tile([P, T], I32, name="word_table")
        nc.sync.dma_start(word_table[:], x_words[0].rearrange("p n j -> p (n j)").bitcast(I32))
        wb_raw.append(load_weight(wb, halves[1], "wb_raw1"))
        for first, gate in ((0, gt), (PACK, gi)):
            nc.sync.dma_start(
                gate_rows[first : first + PACK, :].rearrange("t (q r) -> t q r", r=BLOCK_PARTS),
                gate.rearrange("(q t r) o -> t q (r o)", t=PACK, r=BLOCK_PARTS),
            )
        n4_list = load_list(n4, "n4_list")
        n5_list = load_list(n5, "n5_list")
        n3_list = load_list(n3, "n3_list")
        wa_raw = load_weight(wa, slice(0, H), "wa_raw")
        n1_list = load_list(n1, "n1_list")
        n2_list = load_list(n2, "n2_list")
        n6_list = load_list(n6, "n6_list")
        n7_list = load_list(n7, "n7_list")
        ident = keep.tile([P, P], F32, name="ident")
        make_identity(nc, ident[:])

        windows = [keep.tile([P, WIDE], F32, name="window%d" % t) for t in range(PACK)]
        for t in range(PACK):
            nc.vector.memset(windows[t][:, N:], 0.0)

        two_picked = pick_scales(two_list, "two_picked")
        offs_picked = pick_scales(offs_list, "offs_picked")
        two_scales = deal_scales(two_picked, "two_scales")
        offs_scales = deal_scales(offs_picked, "offs_scales")
        wb_codes = keep.tile([P, N], U32, name="wb_codes", align_bytes=64)
        wb_scales = keep.tile([P, N], U8, name="wb_scales", align_bytes=64)
        wb_bf = [
            keep.tile([P, HALF, PACK], BF16, name="wb_bf%d" % half, tag="wb_bf%d" % half, align_bytes=64)
            for half in range(2)
        ]
        for half in range(2):
            round_weight(wb_raw[half][:], wb_bf[half][:])
        two_words = pick_words(two_list, "two_words", "two_words")

        gate_bank = psum.tile([P, N], F32, name="bank")
        nc.tensor.transpose(gate_bank[:, :P], gate_rows[:], ident[:])
        abs_gi = keep.tile([P, PACK], F32, name="abs_gi")
        neg_abs_gi = keep.tile([P, PACK], F32, name="neg_abs_gi", tag="after_nb", align_bytes=64)
        nc.scalar.activation(abs_gi[:], gate_bank[:, PACK : 2 * PACK], ABS)
        nc.scalar.activation(neg_abs_gi[:], abs_gi[:], COPY, scale=-1.0)
        gates = keep.tile([P, 2 * PACK], F32, name="gates")
        nc.scalar.copy(gates[:], gate_bank[:, : 2 * PACK])

        for half in range(2):
            quantise(wb_codes[:, halves[half]], wb_scales[:, halves[half]], wb_bf[half][:])
            acc = product(two_words, two_scales, wb_codes, wb_scales, 0, halves[half])
            nc.scalar.activation(windows[0][:, halves[half]], acc, COPY, scale=neg_abs_gi[:, 0:1])
        offs_words = pick_words(offs_list, "offs_words", "wb_bf1")
        for t in range(1, PACK):
            acc = product(two_words, two_scales, wb_codes, wb_scales, t)
            nc.scalar.activation(windows[t][:, :N], acc, COPY, scale=neg_abs_gi[:, t : t + 1])

        sign_gi = keep.tile([P, PACK], F32, name="sign_gi", tag="after_nb", align_bytes=64)
        flip = keep.tile([P, PACK], F32, name="flip")
        signed_gt = keep.tile([P, PACK], F32, name="signed_gt")
        nc.scalar.activation(sign_gi[:], gates[:, PACK:], SIGN)
        nc.scalar.activation(flip[:], sign_gi[:], SIGN, scale=-1.0, bias=-0.5)
        for t in range(PACK):
            nc.scalar.activation(signed_gt[:, t : t + 1], gates[:, t : t + 1], COPY, scale=flip[:, t : t + 1])

        wa_bf = keep.tile([P, H, PACK], BF16, name="wa_bf", tag="after_nb", align_bytes=64)
        for half in range(2):
            round_weight(wa_raw[:, :, halves[half]], wa_bf[:, halves[half], :])

        sums = [psum.tile([P, PACK, P], F32, name="sums") for blk in range(PACK)]
        for pair in PAIRS:
            at_n4 = {}
            for t in pair:
                at_n4[t] = ring.tile([P, N], F32, name="at_n4")
                nc.vector.tensor_copy(at_n4[t][:], windows[t][:].indirect(n4_list[:]))
            for t in pair:
                if t == LAST:
                    both = keep.tile([P, 2, N], F32, name="both_last", tag="after_nb", align_bytes=64)
                else:
                    both = ring.tile([P, 2, N], F32, name="both", bufs=LAST)
                diff, rest = both[:, 0, :], both[:, 1, :]
                nc.vector.tensor_tensor(diff, windows[t][:].indirect(n5_list[:]), at_n4[t][:], SUB)
                nc.vector.tensor_tensor(rest, windows[t][:].indirect(n3_list[:]), at_n4[t][:], SUB)
                excess = ring.tile([P, N], F32, name="excess")
                nc.scalar.activation(excess[:], diff, RELU, scale=-1.0)
                terms = (windows[t], excess, rest)
                for blk in range(PACK):
                    for place, term in enumerate(terms):
                        nc.tensor.matmul(
                            sums[blk][:, t, :],
                            lhsT=term[:, blk * P : (blk + 1) * P],
                            rhs=ident[:],
                            is_transpose=True,
                            start=(place == 0),
                            stop=(place == len(terms) - 1),
                        )
            if pair == PAIRS[0]:
                wa_codes = keep.tile([P, H], U32, name="wa_codes", align_bytes=64)
                wa_scales = keep.tile([P, H], U8, name="wa_scales", align_bytes=64)
                quantise(wa_codes[:], wa_scales[:], wa_bf[:])
                a_rows = []
                for t in range(PACK):
                    acc = product(offs_words, offs_scales, wa_codes, wa_scales, t)
                    rows = keep.tile([P, H], F32, name="a_rows%d" % t)
                    nc.scalar.copy(rows[:], acc)
                    a_rows.append(rows)

        z2_bf = keep.tile([P, N, PACK], BF16, name="z2_bf", align_bytes=64)
        z2_pairs = z2_bf[:].rearrange("p c t -> p (c t)").bitcast(F32)
        for half in range(2):
            back = psum.tile([P, N], F32, name="bank")
            for sub in range(2):
                blk = 2 * half + sub
                turned = keep.tile([P, 2, P, 2], BF16, name="turned", tag="turned%d" % blk, align_bytes=64)
                nc.scalar.copy(turned[:], sums[blk][:].rearrange("c (u v) p -> c u p v", v=2))
                turned_pairs = turned[:].rearrange("c u p v -> c (u p v)").bitcast(F32)
                for u in range(2):
                    nc.tensor.transpose(
                        back[:, (2 * sub + u) * P : (2 * sub + u + 1) * P], turned_pairs[:, u * P : (u + 1) * P], ident[:]
                    )
            nc.scalar.copy(
                z2_pairs[:, half * N : (half + 1) * N].rearrange("p (b c u) -> p b c u", b=2, u=2),
                back[:].rearrange("p (b u c) -> p b c u", b=2, u=2),
            )

        z_bf = [
            keep.tile([P, P, PACK], BF16, name="z_bf%d" % e, tag="turned%d" % e, align_bytes=64) for e in range(PACK)
        ]
        for pair in PAIRS:
            pa, pb, dt = {}, {}, {}
            for t in pair:
                pa[t] = ring.tile([P, HALF], F32, name="pa")
                nc.vector.tensor_copy(pa[t][:], a_rows[t][:].indirect(n1_list[:]))
                if t == LAST:
                    pb[t] = keep.tile([P, HALF], F32, name="pb_last", tag="after_scatter", align_bytes=64)
                else:
                    pb[t] = ring.tile([P, HALF], F32, name="pb")
                nc.vector.tensor_copy(pb[t][:], a_rows[t][:].indirect(n2_list[:]))
            for t in pair:
                dt[t] = ring.tile([P, H], F32, name="dt")
                nc.vector.tensor_tensor(dt[t][:].indirect(n1_list[:]), pa[t][:], pb[t][:], ADD)
            for t in pair:
                nc.vector.tensor_tensor(dt[t][:].indirect(n2_list[:]), pa[t][:], pb[t][:], MULT)
                by_residue = dt[t][:].rearrange("p (m e) -> p e m", e=PACK)
                for e in range(PACK):
                    nc.scalar.activation(z_bf[e][:, :, t], by_residue[:, e, :], COPY, scale=signed_gt[:, t : t + 1])

        z2_codes = keep.tile([P, N], U32, name="z2_codes", tag="after_scatter", align_bytes=64)
        z2_scales = keep.tile([P, N], U8, name="z2_scales", align_bytes=64)
        quantise(z2_codes[:], z2_scales[:], z2_bf[:])
        z_codes = keep.tile([P, H], U32, name="z_codes", align_bytes=64)
        z_scales = keep.tile([P, H], U8, name="z_scales", align_bytes=64)
        neg_cv = [keep.tile([P, N], F32, name="neg_cv%d" % e) for e in range(PACK)]
        for e in range(PACK):
            quantise(z_codes[:, e * P : (e + 1) * P], z_scales[:, e * P : (e + 1) * P], z_bf[e][:])
            if e == 0:
                left = product(z_codes, z_scales, z2_codes, z2_scales, e, halves[0])
                right = product(z_codes, z_scales, z2_codes, z2_scales, e, halves[1])
                nc.vector.tensor_scalar_mul(windows[e][:, halves[0]], left, PAIR_SCALE * CV_SCALE)
                nc.vector.tensor_scalar_mul(neg_cv[e][:, halves[0]], left, -CV_SCALE)
                nc.scalar.activation(windows[e][:, halves[1]], right, COPY, scale=PAIR_SCALE * CV_SCALE)
                nc.scalar.activation(neg_cv[e][:, halves[1]], right, COPY, scale=-CV_SCALE)
            else:
                acc = product(z_codes, z_scales, z2_codes, z2_scales, e, tag="sums")
                nc.scalar.activation(windows[e][:, :N], acc, COPY, scale=PAIR_SCALE * CV_SCALE)
                nc.scalar.activation(neg_cv[e][:], acc, COPY, scale=-CV_SCALE)

        out_rows = out.rearrange("(p e) n -> e p n", e=PACK)
        for pair in PAIRS:
            part = {}
            for e in pair:
                part[e] = ring.tile([P, N], F32, name="part")
                nc.vector.tensor_tensor(part[e][:], windows[e][:].indirect(n6_list[:]), neg_cv[e][:], ADD)
            for e in pair:
                pieces = halves if e == LAST else [slice(0, N)]
                for cols in pieces:
                    res = ring.tile([P, cols.stop - cols.start], F32, name="res", bufs=3)
                    entries = n7_list[:, cols.start // PER_COLUMN : cols.stop // PER_COLUMN]
                    nc.vector.tensor_tensor(res[:], windows[e][:].indirect(entries), part[e][:, cols], ADD)
                    nc.sync.dma_start(out_rows[e][:, cols], res[:])
